import numpy as np
import ml_dtypes


def mxq(x, axis, fmt="e4m3"):
    dtype, down = {"e4m3": (ml_dtypes.float8_e4m3fn, 7), "e5m2": (ml_dtypes.float8_e5m2, 14)}[fmt]
    v = np.moveaxis(np.asarray(x, np.float32).astype(ml_dtypes.bfloat16).astype(np.float64), axis, -1)
    blocks = v.reshape(v.shape[:-1] + (-1, 32))
    amax = np.abs(blocks).max(-1, keepdims=True)
    byte = np.maximum(np.where(amax > 0, np.frexp(amax)[1] - 1 + 127, 0) - down, 1)
    scale = np.exp2(byte - 127.0)
    codes = (blocks / scale).astype(np.float32).astype(dtype).astype(np.float64)
    return np.moveaxis((codes * scale).reshape(v.shape), -1, axis)


WIDE = False


def mx_kscale(k):
    if not WIDE:
        return np.ones(k)
    levels = np.array([10, -10, 5, -5, 0])
    if k % 512:
        return np.exp2(np.random.permutation(np.resize(levels, k // 32))).repeat(32)
    a = np.empty((k // 512, 16))
    for p in range(k // 512):
        a[p, :8] = np.random.permutation(np.resize(levels, 8))
        for g in range(8):
            far = levels[np.abs(levels - a[p, g]) >= 10]
            a[p, g + 8] = far[np.random.randint(len(far))]
    return np.exp2(a.ravel()).repeat(32)


def f64(x):
    return np.asarray(x).astype(np.float64)


def striped(idx):
    return np.tile(idx.reshape(-1, 16).T, (8, 1)).astype(np.uint16)


def unstriped(offs):
    return offs[:16].T.reshape(-1).astype(np.int64)


def striped8(idx):
    return np.concatenate([x.reshape(-1, 16).T for x in idx]).astype(np.uint16)


def runs(offs, k):
    lists = np.stack([offs[16 * r : 16 * r + 16].T.reshape(-1) for r in range(8)]).astype(np.int64)
    return lists[np.arange(k) % 512 // 64]


def pack_weight(w):
    k, n = w.shape
    w = f64(np.asarray(w, np.float32).astype(ml_dtypes.bfloat16)).reshape(k // 32, 32, n)
    amax = np.abs(w).max(1)
    byte = np.clip(np.where(amax > 0, np.frexp(amax)[1] - 1 + 127 - 7, 1), 1, 254)
    scaled = (w * np.exp2(127.0 - byte)[:, None, :]).reshape(k, n).astype(np.float32)
    words = np.ascontiguousarray(scaled.reshape(k // 512, 128, 4, n).transpose(0, 1, 3, 2)).astype(ml_dtypes.float8_e4m3fn).view(np.uint8)
    return words, np.ascontiguousarray(byte.astype(np.uint8).reshape(k // 512, 16, n))


def unpack_weight(words, scales):
    g, p, n, _ = words.shape
    vals = np.ascontiguousarray(words).view(ml_dtypes.float8_e4m3fn).astype(np.float64) * np.repeat(np.exp2(scales.astype(np.float64) - 127.0), 8, axis=1)[..., None]
    return vals.transpose(0, 1, 3, 2).reshape(g * 512, n)


def sigmoid(v):
    return 1.0 / (1.0 + np.exp(-np.maximum(v, -700.0)))


K, T, S, N, G, H, W = 512, 1024, 512, 512, 2048, 512, 256


def setup_inputs():
    n = np.random.standard_normal
    s = mx_kscale(K)[:, None]
    u = mx_kscale(S)
    packed_xT = pack_weight(n((K, T)) * s)
    packed_dT = pack_weight(n((K, G)) / s)
    perm = np.random.permutation(S)
    return {
        "x_words": packed_xT[0],
        "x_scales": packed_xT[1],
        "d_words": packed_dT[0],
        "d_scales": packed_dT[1],
        "sl": np.random.uniform(1.0, 2.0, (H, 1)).astype(np.float32),
        "th": (0.5 * n((H, 1))).astype(np.float32),
        "gn": (np.random.uniform(0.5, 1.5, (H, 1)) * u[:, None]).astype(np.float32),
        "gm": (np.random.uniform(0.5, 1.5, (H, 1)) * u[:, None]).astype(np.float32),
        "w1": (n((H, N)) / np.sqrt(2 * H) / u[:, None]).astype(np.float32),
        "w2": (n((H, N)) / np.sqrt(2 * H) / u[:, None]).astype(np.float32),
        "offs": striped(np.random.permutation(T)[:S]),
        "k1": striped8(np.random.randint(0, G, (8, H))),
        "two": striped(np.random.permutation(T)[:S]),
        "n1": striped(np.random.permutation(S)),
        "n2": striped(np.random.permutation(S)),
        "n3": striped(perm[:W]),
        "n4": striped(perm[W:]),
        "n5": striped(np.random.permutation(S)),
    }


def reference(x_words, x_scales, d_words, d_scales, sl, th, gn, gm, w1, w2, offs, k1, two, n1, n2, n3, n4, n5):
    d_k1 = unpack_weight(d_words, d_scales)[np.arange(K)[:, None], runs(k1, K)]
    xq = unpack_weight(x_words, x_scales)[:, unstriped(offs)]
    a = 0.0625 * (d_k1.T @ xq)
    st = a - a[:, unstriped(n1)]
    sg = sigmoid(f64(sl) * (st[:, unstriped(n2)] - f64(th)))
    z = f64(gn) * (a * sg)
    x_two = unpack_weight(x_words, x_scales)[:, unstriped(two)]
    b = 0.0625 * (d_k1.T @ x_two)
    pb = b[:, unstriped(n4)]
    pa = b[:, unstriped(n3)]
    rb = pb * sigmoid(pb - pa)
    ra = pa * sigmoid(pa - pb)
    ds = np.zeros((H, S))
    ds[:, unstriped(n3)] = ra
    dt = ds.copy()
    dt[:, unstriped(n4)] = rb
    z2 = f64(gm) * dt
    h = mxq(f64(w1), 0, "e4m3").T @ mxq(z, 0, "e4m3") + mxq(f64(w2), 0, "e4m3").T @ mxq(z2, 0, "e4m3")
    return h / (np.abs(h[:, unstriped(n5)]) + 0.5)

@@ -1,0 +1,216 @@
+from contextlib import ExitStack
+
+import concourse.mybir as mybir
+
+K, T, S, N, G, H, W = 512, 1024, 512, 512, 2048, 512, 256
+FLOPS = 4 * 2 * 512 * 512 * 512
+
+F32 = mybir.dt.float32
+BF16 = mybir.dt.bfloat16
+I32 = mybir.dt.int32
+U32 = mybir.dt.uint32
+U16 = mybir.dt.uint16
+U8 = mybir.dt.uint8
+FP8X4 = mybir.dt.float8_e4m3fn_x4
+ALU = mybir.AluOpType
+ACT = mybir.ActivationFunctionType
+
+P = 128
+PACK = 4
+SPARE = 192
+SCORE_SCALE = 0.0625
+
+
+def tile_picked_kjehqduelnorm_none_p_kernel(
+    tc, x_words, x_scales, d_words, d_scales, sl, th, gn, gm, w1, w2, offs, k1, two, n1, n2, n3, n4, n5, out
+):
+    nc = tc.nc
+    with ExitStack() as ctx:
+        keep = ctx.enter_context(tc.tile_pool(name="keep", bufs=1))
+        psum = ctx.enter_context(tc.psum_pool(name="psum", bufs=1))
+
+        def load_list(name, src):
+            tile = keep.tile(list(src.shape), U16, name=name)
+            nc.sync.dma_start(tile[:], src)
+            return tile
+
+        def load_words(name, src, width):
+            tile = keep.tile([P, width], U32, name=name, align_bytes=64)
+            nc.sync.dma_start(tile[:].bitcast(I32), src[0].rearrange("p n r -> p (n r)").bitcast(I32))
+            return tile
+
+        def zeroed_bytes(name, width, engine):
+            tile = keep.tile([P, width], U8, name=name, align_bytes=64)
+            engine.memset(tile[:].bitcast(I32), 0)
+            return tile
+
+        def load_rows(name, src):
+            tile = keep.tile([P, PACK], F32, name=name)
+            nc.sync.dma_start(tile[:], src.rearrange("(p t) o -> p (t o)", t=PACK))
+            return tile
+
+        def load_weight(name, src):
+            tile = keep.tile([P, PACK, N], F32, name=name)
+            nc.sync.dma_start(tile[:], src.rearrange("(p t) m -> p t m", t=PACK))
+            return tile
+
+        def gather(name, table, offsets, dtype):
+            tile = keep.tile([P, S], dtype, name=name, align_bytes=64)
+            nc.vector.tensor_copy(tile[:], table[:].indirect(offsets[:]))
+            return tile
+
+        def deal(name, src, dtype):
+            tile = keep.tile([P, H], dtype, name=name, align_bytes=64)
+            nc.vector.tensor_copy(
+                tile[:].rearrange("p (t m) -> p t m", t=PACK), src[:].rearrange("p (m t) -> p t m", t=PACK)
+            )
+            return tile
+
+        def interleave(name, planes, copy):
+            tile = keep.tile([P, S, PACK], BF16, name=name, align_bytes=64)
+            copy(tile[:].rearrange("p (c i) t -> p c t i", i=4), planes[:].rearrange("p t (c i) -> p c t i", i=4))
+            return tile
+
+        def quantize(name, grouped):
+            codes = keep.tile([P, S], U32, name=name + "_codes", align_bytes=64)
+            scales = keep.tile([P, S], U8, name=name + "_scales", align_bytes=64)
+            nc.vector.quantize_mx(
+                out=codes[:].bitcast(FP8X4), scales=scales[:], in_=grouped[:].rearrange("p c t -> p (c t)")
+            )
+            return codes, scales
+
+        def product(bank, lhs, t, rhs, start, stop):
+            cols = slice(t * P, (t + 1) * P)
+            nc.tensor.matmul_mx(
+                out=bank[:],
+                lhsT=lhs[0][:, cols].bitcast(FP8X4),
+                lhsT_scale=lhs[1][:, cols],
+                rhs=rhs[0][:].bitcast(FP8X4),
+                rhs_scale=rhs[1][:],
+                start=start,
+                stop=stop,
+            )
+
+        d_scale_table = zeroed_bytes("d_scale_table", G, nc.vector)
+        x_scale_table = zeroed_bytes("x_scale_table", T, nc.gpsimd)
+        key_scales = zeroed_bytes("key_scales", H, nc.gpsimd)
+        nc.scalar.dma_start(d_scale_table[0:P:8, :].bitcast(I32), d_scales[0].bitcast(I32))
+        for q in range(4):
+            nc.scalar.dma_start(
+                x_scale_table[32 * q : 32 * q + 4, :].bitcast(I32), x_scales[0, 4 * q : 4 * q + 4, :].bitcast(I32)
+            )
+        k1_t = load_list("k1_t", k1)
+        d_table = load_words("d_table", d_words, G)
+        two_t = load_list("two_t", two)
+        x_table = load_words("x_table", x_words, T)
+        offs_t = load_list("offs_t", offs)
+        n3_t = load_list("n3_t", n3)
+        n4_t = load_list("n4_t", n4)
+        n1_t = load_list("n1_t", n1)
+        w1_raw = load_weight("w1_raw", w1)
+        sl_t = load_rows("sl_t", sl)
+        th_t = load_rows("th_t", th)
+        n2_t = load_list("n2_t", n2)
+        gn_t = load_rows("gn_t", gn)
+        gm_t = load_rows("gm_t", gm)
+        n5_t = load_list("n5_t", n5)
+        w2_raw = load_weight("w2_raw", w2)
+
+        key_scales_dealt = deal("key_scales_dealt", gather("key_scales_picked", d_scale_table, k1_t, U8), U8)
+        for r in range(4):
+            nc.scalar.dma_start(
+                key_scales[r:P:32, :].bitcast(I32), key_scales_dealt[8 * r : P : 32, :].bitcast(I32)
+            )
+        keys = (deal("key_codes", gather("key_codes_picked", d_table, k1_t, U32), U32), key_scales)
+        xb = (gather("xb_codes", x_table, two_t, U32), gather("xb_scales", x_scale_table, two_t, U8))
+        b_banks = [psum.tile([P, S], F32, name=f"b_bank{t}", tag=f"late{t}") for t in range(PACK)]
+        for t in range(PACK):
+            product(b_banks[t], keys, t, xb, True, True)
+        xa = (gather("xa_codes", x_table, offs_t, U32), gather("xa_scales", x_scale_table, offs_t, U8))
+        a_banks = [psum.tile([P, S], F32, name=f"a_bank{t}") for t in range(PACK)]
+        for t in range(PACK):
+            product(a_banks[t], keys, t, xa, True, True)
+
+        def round_weight(name, raw):
+            tile = keep.tile([P, N, PACK], BF16, name=name, align_bytes=64)
+            nc.gpsimd.tensor_scalar(tile[:], raw[:].rearrange("p t m -> p m t"), 1.0, 0.0, ALU.mult, ALU.add)
+            return tile
+
+        w1_grouped = round_weight("w1_grouped", w1_raw)
+        w2_grouped = round_weight("w2_grouped", w2_raw)
+
+        sg_bias = keep.tile([P, PACK], F32, name="sg_bias")
+        nc.vector.scalar_tensor_tensor(sg_bias[:], sl_t[:], -1.0, th_t[:], ALU.mult, ALU.mult)
+        z_gain = keep.tile([P, PACK], F32, name="z_gain")
+        nc.vector.tensor_scalar(z_gain[:], gn_t[:], SCORE_SCALE, None, ALU.mult)
+
+        z_planes = keep.tile([P, PACK, S], BF16, name="z_planes", align_bytes=64)
+        z2_planes = keep.tile([P, PACK, S], BF16, name="z2_planes", align_bytes=64)
+
+        def rows(name, shape):
+            return [keep.tile([P] + shape, F32, name=f"{name}{t}") for t in range(PACK)]
+
+        b_row, pair, lead, share = rows("b_row", [S]), rows("pair", [2, W]), rows("lead", [W]), rows("share", [2, W])
+        rb, dt = rows("rb", [W]), rows("dt", [S])
+        a_row, st, sg = rows("a_row", [S + SPARE]), rows("st", [2 * S]), rows("sg", [S])
+
+        def fetch(t):
+            nc.scalar.activation(b_row[t][:], b_banks[t][:], ACT.Copy, scale=SCORE_SCALE)
+            nc.vector.tensor_copy(pair[t][:, 0, :], b_row[t][:].indirect(n3_t[:]))
+            nc.scalar.activation(pair[t][:, 1, :], b_row[t][:].indirect(n4_t[:]), ACT.Copy)
+            nc.vector.tensor_tensor(lead[t][:], pair[t][:, 0, :], pair[t][:, 1, :], ALU.subtract)
+            nc.scalar.activation(share[t][:, 0, :], lead[t][:], ACT.Sigmoid)
+            nc.scalar.activation(share[t][:, 1, :], lead[t][:], ACT.Sigmoid, scale=-1.0)
+            nc.scalar.activation(a_row[t][:, :S], a_banks[t][:], ACT.Copy, scale=SCORE_SCALE)
+            nc.vector.tensor_copy(st[t][:, S:], a_row[t][:].indirect(n1_t[:]))
+
+        def combine(t):
+            nc.vector.tensor_tensor(rb[t][:], pair[t][:, 1, :], share[t][:, 1, :], ALU.mult)
+            nc.vector.scalar_tensor_tensor(
+                st[t][:, :S], a_banks[t][:], SCORE_SCALE, st[t][:, S:], ALU.mult, ALU.subtract
+            )
+
+        def place(t):
+            nc.scalar.activation(
+                sg[t][:], st[t][:].indirect(n2_t[:]), ACT.Sigmoid, bias=sg_bias[:, t : t + 1], scale=sl_t[:, t : t + 1]
+            )
+            nc.vector.tensor_tensor(dt[t][:].indirect(n3_t[:]), pair[t][:, 0, :], share[t][:, 0, :], ALU.mult)
+            nc.scalar.activation(dt[t][:].indirect(n4_t[:]), rb[t][:], ACT.Copy)
+
+        def round_once(t):
+            nc.vector.scalar_tensor_tensor(
+                z_planes[:, t, :], a_banks[t][:], z_gain[:, t : t + 1], sg[t][:], ALU.mult, ALU.mult
+            )
+            nc.vector.tensor_scalar(z2_planes[:, t, :], dt[t][:], gm_t[:, t : t + 1], None, ALU.mult)
+
+        stages = (fetch, combine, place, round_once)
+        for step in range(PACK + len(stages) - 1):
+            for lag, stage in enumerate(stages):
+                if 0 <= step - lag < PACK:
+                    stage(step - lag)
+            if step == 2:
+                w1_q = quantize("w1", w1_grouped)
+            if step == 3:
+                w2_q = quantize("w2", w2_grouped)
+
+        z_q = quantize("z", interleave("z_grouped", z_planes, nc.vector.tensor_copy))
+        z2_q = quantize("z2", interleave("z2_grouped", z2_planes, nc.scalar.copy))
+
+        h_banks = [psum.tile([P, S], F32, name=f"h_bank{t}", tag=f"late{t}") for t in range(PACK)]
+        for t in range(PACK):
+            product(h_banks[t], w1_q, t, z_q, True, False)
+        for t in range(PACK):
+            product(h_banks[t], w2_q, t, z2_q, False, True)
+
+        size, picked = rows("size", [S + SPARE]), rows("picked", [S])
+        root, inverse, result = rows("root", [S]), rows("inverse", [S]), rows("result", [S])
+        for t in range(PACK):
+            nc.scalar.activation(size[t][:, :S], h_banks[t][:], ACT.Abs)
+        for t in range(PACK):
+            nc.vector.tensor_copy(picked[t][:], size[t][:].indirect(n5_t[:]))
+        for t in range(PACK):
+            nc.scalar.activation(root[t][:], picked[t][:], ACT.Abs_reciprocal_sqrt, bias=0.5)
+            nc.scalar.activation(inverse[t][:], root[t][:], ACT.Square)
+        for t in range(PACK):
+            nc.vector.tensor_tensor(result[t][:], h_banks[t][:], inverse[t][:], ALU.mult)
+            nc.sync.dma_start(out[t * P : (t + 1) * P, :], result[t][:])

@@ -19,6 +19,8 @@ P = 128
 PACK = 4
 SPARE = 192
 SCORE_SCALE = 0.0625
+A_LAG = 3
+SPLIT = 336
 
 
 def tile_picked_kjehqduelnorm_none_p_kernel(
@@ -49,13 +51,13 @@ def tile_picked_kjehqduelnorm_none_p_kernel(
             nc.sync.dma_start(tile[:], src.rearrange("(p t) o -> p (t o)", t=PACK))
             return tile
 
-        def load_weight(name, src):
-            tile = keep.tile([P, PACK, N], F32, name=name)
+        def load_weight(name, src, tag=""):
+            tile = keep.tile([P, PACK, N], F32, name=name, tag=tag, align_bytes=64)
             nc.sync.dma_start(tile[:], src.rearrange("(p t) m -> p t m", t=PACK))
             return tile
 
-        def gather(name, table, offsets, dtype):
-            tile = keep.tile([P, S], dtype, name=name, align_bytes=64)
+        def gather(name, table, offsets, dtype, tag=""):
+            tile = keep.tile([P, S], dtype, name=name, tag=tag, align_bytes=64)
             nc.vector.tensor_copy(tile[:], table[:].indirect(offsets[:]))
             return tile
 
@@ -66,9 +68,13 @@ def tile_picked_kjehqduelnorm_none_p_kernel(
             )
             return tile
 
-        def interleave(name, planes, copy):
+        def interleave(name, planes, shares):
             tile = keep.tile([P, S, PACK], BF16, name=name, align_bytes=64)
-            copy(tile[:].rearrange("p (c i) t -> p c t i", i=4), planes[:].rearrange("p t (c i) -> p c t i", i=4))
+            for copy, cols in shares:
+                copy(
+                    tile[:, cols, :].rearrange("p (c i) t -> p c t i", i=4),
+                    planes[:, :, cols].rearrange("p t (c i) -> p c t i", i=4),
+                )
             return tile
 
         def quantize(name, grouped):
@@ -91,53 +97,59 @@ def tile_picked_kjehqduelnorm_none_p_kernel(
                 stop=stop,
             )
 
-        d_scale_table = zeroed_bytes("d_scale_table", G, nc.vector)
+        on_scalar = [(nc.scalar.copy, slice(0, S))]
+        on_vector = [(nc.vector.tensor_copy, slice(0, S))]
+        on_both = [(nc.vector.tensor_copy, slice(0, SPLIT)), (nc.scalar.copy, slice(SPLIT, S))]
+
+        d_scale_table = zeroed_bytes("d_scale_table", G, nc.gpsimd)
         x_scale_table = zeroed_bytes("x_scale_table", T, nc.gpsimd)
         key_scales = zeroed_bytes("key_scales", H, nc.gpsimd)
-        nc.scalar.dma_start(d_scale_table[0:P:8, :].bitcast(I32), d_scales[0].bitcast(I32))
+        two_t = load_list("two_t", two)
+        k1_t = load_list("k1_t", k1)
+        x_table = load_words("x_table", x_words, T)
+        nc.sync.dma_start(d_scale_table[0:P:8, :].bitcast(I32), d_scales[0].bitcast(I32))
+        d_table = load_words("d_table", d_words, G)
         for q in range(4):
             nc.scalar.dma_start(
                 x_scale_table[32 * q : 32 * q + 4, :].bitcast(I32), x_scales[0, 4 * q : 4 * q + 4, :].bitcast(I32)
             )
-        k1_t = load_list("k1_t", k1)
-        d_table = load_words("d_table", d_words, G)
-        two_t = load_list("two_t", two)
-        x_table = load_words("x_table", x_words, T)
+        sigmoid_warm = keep.tile([P, 2], F32, name="sigmoid_warm")
+        nc.gpsimd.memset(sigmoid_warm[:, 0:1], 0.0)
+        nc.scalar.activation(sigmoid_warm[:, 1:2], sigmoid_warm[:, 0:1], ACT.Sigmoid)
+        w1_raw = load_weight("w1_raw", w1)
         offs_t = load_list("offs_t", offs)
         n3_t = load_list("n3_t", n3)
         n4_t = load_list("n4_t", n4)
-        n1_t = load_list("n1_t", n1)
-        w1_raw = load_weight("w1_raw", w1)
-        sl_t = load_rows("sl_t", sl)
-        th_t = load_rows("th_t", th)
-        n2_t = load_list("n2_t", n2)
-        gn_t = load_rows("gn_t", gn)
-        gm_t = load_rows("gm_t", gm)
-        n5_t = load_list("n5_t", n5)
-        w2_raw = load_weight("w2_raw", w2)
 
         key_scales_dealt = deal("key_scales_dealt", gather("key_scales_picked", d_scale_table, k1_t, U8), U8)
         for r in range(4):
             nc.scalar.dma_start(
                 key_scales[r:P:32, :].bitcast(I32), key_scales_dealt[8 * r : P : 32, :].bitcast(I32)
             )
+        w2_raw = load_weight("w2_raw", w2, tag="key_scales_picked")
+        n1_t = load_list("n1_t", n1)
+        sl_t = load_rows("sl_t", sl)
+        th_t = load_rows("th_t", th)
+        n2_t = load_list("n2_t", n2)
+        gn_t = load_rows("gn_t", gn)
+        gm_t = load_rows("gm_t", gm)
+        n5_t = load_list("n5_t", n5)
         keys = (deal("key_codes", gather("key_codes_picked", d_table, k1_t, U32), U32), key_scales)
         xb = (gather("xb_codes", x_table, two_t, U32), gather("xb_scales", x_scale_table, two_t, U8))
         b_banks = [psum.tile([P, S], F32, name=f"b_bank{t}", tag=f"late{t}") for t in range(PACK)]
         for t in range(PACK):
             product(b_banks[t], keys, t, xb, True, True)
-        xa = (gather("xa_codes", x_table, offs_t, U32), gather("xa_scales", x_scale_table, offs_t, U8))
+        xa = (
+            gather("xa_codes", x_table, offs_t, U32, tag="key_codes_picked"),
+            gather("xa_scales", x_scale_table, offs_t, U8, tag="key_scales_dealt"),
+        )
         a_banks = [psum.tile([P, S], F32, name=f"a_bank{t}") for t in range(PACK)]
         for t in range(PACK):
             product(a_banks[t], keys, t, xa, True, True)
 
-        def round_weight(name, raw):
-            tile = keep.tile([P, N, PACK], BF16, name=name, align_bytes=64)
-            nc.gpsimd.tensor_scalar(tile[:], raw[:].rearrange("p t m -> p m t"), 1.0, 0.0, ALU.mult, ALU.add)
-            return tile
-
-        w1_grouped = round_weight("w1_grouped", w1_raw)
-        w2_grouped = round_weight("w2_grouped", w2_raw)
+        w1_grouped = interleave("w1_grouped", w1_raw, on_scalar)
+        w2_grouped = keep.tile([P, N, PACK], BF16, name="w2_grouped", align_bytes=64)
+        nc.gpsimd.tensor_scalar(w2_grouped[:], w2_raw[:].rearrange("p t m -> p m t"), 1.0, 0.0, ALU.mult, ALU.add)
 
         sg_bias = keep.tile([P, PACK], F32, name="sg_bias")
         nc.vector.scalar_tensor_tensor(sg_bias[:], sl_t[:], -1.0, th_t[:], ALU.mult, ALU.mult)
@@ -154,53 +166,65 @@ def tile_picked_kjehqduelnorm_none_p_kernel(
         rb, dt = rows("rb", [W]), rows("dt", [S])
         a_row, st, sg = rows("a_row", [S + SPARE]), rows("st", [2 * S]), rows("sg", [S])
 
-        def fetch(t):
+        def fetch_pairs(t):
             nc.scalar.activation(b_row[t][:], b_banks[t][:], ACT.Copy, scale=SCORE_SCALE)
             nc.vector.tensor_copy(pair[t][:, 0, :], b_row[t][:].indirect(n3_t[:]))
             nc.scalar.activation(pair[t][:, 1, :], b_row[t][:].indirect(n4_t[:]), ACT.Copy)
-            nc.vector.tensor_tensor(lead[t][:], pair[t][:, 0, :], pair[t][:, 1, :], ALU.subtract)
+
+        def weigh_pairs(t):
+            nc.gpsimd.tensor_tensor(lead[t][:], pair[t][:, 0, :], pair[t][:, 1, :], ALU.subtract)
             nc.scalar.activation(share[t][:, 0, :], lead[t][:], ACT.Sigmoid)
             nc.scalar.activation(share[t][:, 1, :], lead[t][:], ACT.Sigmoid, scale=-1.0)
+
+        def place_pairs(t):
+            nc.gpsimd.tensor_tensor(rb[t][:], pair[t][:, 1, :], share[t][:, 1, :], ALU.mult)
+            nc.vector.tensor_tensor(dt[t][:].indirect(n3_t[:]), pair[t][:, 0, :], share[t][:, 0, :], ALU.mult)
+            nc.scalar.activation(dt[t][:].indirect(n4_t[:]), rb[t][:], ACT.Copy)
+
+        def round_z2(t):
+            nc.gpsimd.tensor_scalar(z2_planes[:, t, :], dt[t][:], gm_t[:, t : t + 1], 0.0, ALU.mult, ALU.add)
+
+        def fetch_a(t):
             nc.scalar.activation(a_row[t][:, :S], a_banks[t][:], ACT.Copy, scale=SCORE_SCALE)
             nc.vector.tensor_copy(st[t][:, S:], a_row[t][:].indirect(n1_t[:]))
 
-        def combine(t):
-            nc.vector.tensor_tensor(rb[t][:], pair[t][:, 1, :], share[t][:, 1, :], ALU.mult)
+        def make_st(t):
             nc.vector.scalar_tensor_tensor(
                 st[t][:, :S], a_banks[t][:], SCORE_SCALE, st[t][:, S:], ALU.mult, ALU.subtract
             )
 
-        def place(t):
+        def make_sg(t):
             nc.scalar.activation(
                 sg[t][:], st[t][:].indirect(n2_t[:]), ACT.Sigmoid, bias=sg_bias[:, t : t + 1], scale=sl_t[:, t : t + 1]
             )
-            nc.vector.tensor_tensor(dt[t][:].indirect(n3_t[:]), pair[t][:, 0, :], share[t][:, 0, :], ALU.mult)
-            nc.scalar.activation(dt[t][:].indirect(n4_t[:]), rb[t][:], ACT.Copy)
 
-        def round_once(t):
+        def round_z(t):
             nc.vector.scalar_tensor_tensor(
                 z_planes[:, t, :], a_banks[t][:], z_gain[:, t : t + 1], sg[t][:], ALU.mult, ALU.mult
             )
-            nc.vector.tensor_scalar(z2_planes[:, t, :], dt[t][:], gm_t[:, t : t + 1], None, ALU.mult)
 
-        stages = (fetch, combine, place, round_once)
-        for step in range(PACK + len(stages) - 1):
-            for lag, stage in enumerate(stages):
+        b_stages = list(enumerate((fetch_pairs, weigh_pairs, place_pairs, round_z2)))
+        a_stages = list(enumerate((fetch_a, make_st, make_sg, round_z), A_LAG))
+        for step in range(A_LAG + 2 * PACK - 1):
+            for lag, stage in b_stages + a_stages:
                 if 0 <= step - lag < PACK:
                     stage(step - lag)
             if step == 2:
                 w1_q = quantize("w1", w1_grouped)
-            if step == 3:
                 w2_q = quantize("w2", w2_grouped)
+            if step == 2 * PACK - 2:
+                z2_q = quantize("z2", interleave("z2_grouped", z2_planes, on_vector))
 
-        z_q = quantize("z", interleave("z_grouped", z_planes, nc.vector.tensor_copy))
-        z2_q = quantize("z2", interleave("z2_grouped", z2_planes, nc.scalar.copy))
+        z_grouped = interleave("z_grouped", z_planes, on_both)
+        root_warm = keep.tile([P, 1], F32, name="root_warm")
+        nc.scalar.activation(root_warm[:], z_grouped[:, S - 1, 0:1], ACT.Abs_reciprocal_sqrt, bias=0.5, scale=0.0)
+        z_q = quantize("z", z_grouped)
 
         h_banks = [psum.tile([P, S], F32, name=f"h_bank{t}", tag=f"late{t}") for t in range(PACK)]
         for t in range(PACK):
-            product(h_banks[t], w1_q, t, z_q, True, False)
+            product(h_banks[t], w2_q, t, z2_q, True, False)
         for t in range(PACK):
-            product(h_banks[t], w2_q, t, z2_q, False, True)
+            product(h_banks[t], w1_q, t, z_q, False, True)
 
         size, picked = rows("size", [S + SPARE]), rows("picked", [S])
         root, inverse, result = rows("root", [S]), rows("inverse", [S]), rows("result", [S])

@@ -148,8 +148,6 @@ def tile_picked_kjehqduelnorm_none_p_kernel(
             product(a_banks[t], keys, t, xa, True, True)
 
         w1_grouped = interleave("w1_grouped", w1_raw, on_scalar)
-        w2_grouped = keep.tile([P, N, PACK], BF16, name="w2_grouped", align_bytes=64)
-        nc.gpsimd.tensor_scalar(w2_grouped[:], w2_raw[:].rearrange("p t m -> p m t"), 1.0, 0.0, ALU.mult, ALU.add)
 
         sg_bias = keep.tile([P, PACK], F32, name="sg_bias")
         nc.vector.scalar_tensor_tensor(sg_bias[:], sl_t[:], -1.0, th_t[:], ALU.mult, ALU.mult)
@@ -163,32 +161,37 @@ def tile_picked_kjehqduelnorm_none_p_kernel(
             return [keep.tile([P] + shape, F32, name=f"{name}{t}") for t in range(PACK)]
 
         b_row, pair, lead, share = rows("b_row", [S]), rows("pair", [2, W]), rows("lead", [W]), rows("share", [2, W])
-        rb, dt = rows("rb", [W]), rows("dt", [S])
+        won, dt = rows("won", [2, W]), rows("dt", [S])
         a_row, st, sg = rows("a_row", [S + SPARE]), rows("st", [2 * S]), rows("sg", [S])
 
         def fetch_pairs(t):
             nc.scalar.activation(b_row[t][:], b_banks[t][:], ACT.Copy, scale=SCORE_SCALE)
-            nc.vector.tensor_copy(pair[t][:, 0, :], b_row[t][:].indirect(n3_t[:]))
-            nc.scalar.activation(pair[t][:, 1, :], b_row[t][:].indirect(n4_t[:]), ACT.Copy)
+            for half, offsets in enumerate((n3_t, n4_t)):
+                if t == 0:
+                    nc.scalar.activation(pair[t][:, half, :], b_row[t][:].indirect(offsets[:]), ACT.Copy)
+                else:
+                    nc.vector.tensor_copy(pair[t][:, half, :], b_row[t][:].indirect(offsets[:]))
 
         def weigh_pairs(t):
-            nc.gpsimd.tensor_tensor(lead[t][:], pair[t][:, 0, :], pair[t][:, 1, :], ALU.subtract)
+            nc.vector.tensor_tensor(lead[t][:], pair[t][:, 0, :], pair[t][:, 1, :], ALU.subtract)
             nc.scalar.activation(share[t][:, 0, :], lead[t][:], ACT.Sigmoid)
             nc.scalar.activation(share[t][:, 1, :], lead[t][:], ACT.Sigmoid, scale=-1.0)
 
         def place_pairs(t):
-            nc.gpsimd.tensor_tensor(rb[t][:], pair[t][:, 1, :], share[t][:, 1, :], ALU.mult)
-            nc.vector.tensor_tensor(dt[t][:].indirect(n3_t[:]), pair[t][:, 0, :], share[t][:, 0, :], ALU.mult)
-            nc.scalar.activation(dt[t][:].indirect(n4_t[:]), rb[t][:], ACT.Copy)
+            if t == 0:
+                nc.vector.tensor_tensor(won[t][:], pair[t][:], share[t][:], ALU.mult)
+                nc.scalar.activation(dt[t][:].indirect(n3_t[:]), won[t][:, 0, :], ACT.Copy)
+            else:
+                nc.vector.tensor_tensor(won[t][:, 1, :], pair[t][:, 1, :], share[t][:, 1, :], ALU.mult)
+                nc.vector.tensor_tensor(dt[t][:].indirect(n3_t[:]), pair[t][:, 0, :], share[t][:, 0, :], ALU.mult)
+            nc.scalar.activation(dt[t][:].indirect(n4_t[:]), won[t][:, 1, :], ACT.Copy)
 
         def round_z2(t):
-            nc.gpsimd.tensor_scalar(z2_planes[:, t, :], dt[t][:], gm_t[:, t : t + 1], 0.0, ALU.mult, ALU.add)
-
-        def fetch_a(t):
-            nc.scalar.activation(a_row[t][:, :S], a_banks[t][:], ACT.Copy, scale=SCORE_SCALE)
-            nc.vector.tensor_copy(st[t][:, S:], a_row[t][:].indirect(n1_t[:]))
+            nc.vector.tensor_scalar(z2_planes[:, t, :], dt[t][:], gm_t[:, t : t + 1], None, ALU.mult)
 
         def make_st(t):
+            nc.scalar.activation(a_row[t][:, :S], a_banks[t][:], ACT.Copy, scale=SCORE_SCALE)
+            nc.vector.tensor_copy(st[t][:, S:], a_row[t][:].indirect(n1_t[:]))
             nc.vector.scalar_tensor_tensor(
                 st[t][:, :S], a_banks[t][:], SCORE_SCALE, st[t][:, S:], ALU.mult, ALU.subtract
             )
@@ -204,16 +207,16 @@ def tile_picked_kjehqduelnorm_none_p_kernel(
             )
 
         b_stages = list(enumerate((fetch_pairs, weigh_pairs, place_pairs, round_z2)))
-        a_stages = list(enumerate((fetch_a, make_st, make_sg, round_z), A_LAG))
-        for step in range(A_LAG + 2 * PACK - 1):
-            for lag, stage in b_stages + a_stages:
+        a_stages = list(enumerate((make_st, make_sg, round_z), A_LAG))
+        for step in range(A_LAG + 2 * PACK - 2):
+            for lag, stage in a_stages + b_stages:
                 if 0 <= step - lag < PACK:
                     stage(step - lag)
             if step == 2:
                 w1_q = quantize("w1", w1_grouped)
-                w2_q = quantize("w2", w2_grouped)
+                w2_q = quantize("w2", interleave("w2_grouped", w2_raw, on_scalar))
             if step == 2 * PACK - 2:
-                z2_q = quantize("z2", interleave("z2_grouped", z2_planes, on_vector))
+                z2_q = quantize("z2", interleave("z2_grouped", z2_planes, on_both))
 
         z_grouped = interleave("z_grouped", z_planes, on_both)
         root_warm = keep.tile([P, 1], F32, name="root_warm")
@@ -230,11 +233,13 @@ def tile_picked_kjehqduelnorm_none_p_kernel(
         root, inverse, result = rows("root", [S]), rows("inverse", [S]), rows("result", [S])
         for t in range(PACK):
             nc.scalar.activation(size[t][:, :S], h_banks[t][:], ACT.Abs)
-        for t in range(PACK):
-            nc.vector.tensor_copy(picked[t][:], size[t][:].indirect(n5_t[:]))
-        for t in range(PACK):
-            nc.scalar.activation(root[t][:], picked[t][:], ACT.Abs_reciprocal_sqrt, bias=0.5)
-            nc.scalar.activation(inverse[t][:], root[t][:], ACT.Square)
-        for t in range(PACK):
-            nc.vector.tensor_tensor(result[t][:], h_banks[t][:], inverse[t][:], ALU.mult)
-            nc.sync.dma_start(out[t * P : (t + 1) * P, :], result[t][:])
+        pieces = [(t, slice(0, S)) for t in range(PACK - 1)] + [(PACK - 1, slice(0, W)), (PACK - 1, slice(W, S))]
+        for t, cols in pieces:
+            offsets = n5_t[:, cols.start // 16 : cols.stop // 16]
+            nc.vector.tensor_copy(picked[t][:, cols], size[t][:].indirect(offsets))
+        for t, cols in pieces:
+            nc.scalar.activation(root[t][:, cols], picked[t][:, cols], ACT.Abs_reciprocal_sqrt, bias=0.5)
+            nc.scalar.activation(inverse[t][:, cols], root[t][:, cols], ACT.Square)
+        for t, cols in pieces:
+            nc.vector.tensor_tensor(result[t][:, cols], h_banks[t][:, cols], inverse[t][:, cols], ALU.mult)
+            nc.sync.dma_start(out[t * P : (t + 1) * P, cols], result[t][:, cols])

from contextlib import ExitStack

import concourse.mybir as mybir

K, T, S, N, G, H, W = 512, 1024, 512, 512, 2048, 512, 256
FLOPS = 4 * 2 * 512 * 512 * 512

F32 = mybir.dt.float32
BF16 = mybir.dt.bfloat16
I32 = mybir.dt.int32
U32 = mybir.dt.uint32
U16 = mybir.dt.uint16
U8 = mybir.dt.uint8
FP8X4 = mybir.dt.float8_e4m3fn_x4
ALU = mybir.AluOpType
ACT = mybir.ActivationFunctionType

P = 128
PACK = 4
SPARE = 192
SCORE_SCALE = 0.0625
A_LAG = 3
SPLIT = 336


def tile_picked_kjehqduelnorm_none_p_kernel(
    tc, x_words, x_scales, d_words, d_scales, sl, th, gn, gm, w1, w2, offs, k1, two, n1, n2, n3, n4, n5, out
):
    nc = tc.nc
    with ExitStack() as ctx:
        keep = ctx.enter_context(tc.tile_pool(name="keep", bufs=1))
        psum = ctx.enter_context(tc.psum_pool(name="psum", bufs=1))

        def load_list(name, src):
            tile = keep.tile(list(src.shape), U16, name=name)
            nc.sync.dma_start(tile[:], src)
            return tile

        def load_words(name, src, width):
            tile = keep.tile([P, width], U32, name=name, align_bytes=64)
            nc.sync.dma_start(tile[:].bitcast(I32), src[0].rearrange("p n r -> p (n r)").bitcast(I32))
            return tile

        def zeroed_bytes(name, width, engine):
            tile = keep.tile([P, width], U8, name=name, align_bytes=64)
            engine.memset(tile[:].bitcast(I32), 0)
            return tile

        def load_rows(name, src):
            tile = keep.tile([P, PACK], F32, name=name)
            nc.sync.dma_start(tile[:], src.rearrange("(p t) o -> p (t o)", t=PACK))
            return tile

        def load_weight(name, src, tag=""):
            tile = keep.tile([P, PACK, N], F32, name=name, tag=tag, align_bytes=64)
            nc.sync.dma_start(tile[:], src.rearrange("(p t) m -> p t m", t=PACK))
            return tile

        def gather(name, table, offsets, dtype, tag=""):
            tile = keep.tile([P, S], dtype, name=name, tag=tag, align_bytes=64)
            nc.vector.tensor_copy(tile[:], table[:].indirect(offsets[:]))
            return tile

        def deal(name, src, dtype):
            tile = keep.tile([P, H], dtype, name=name, align_bytes=64)
            nc.vector.tensor_copy(
                tile[:].rearrange("p (t m) -> p t m", t=PACK), src[:].rearrange("p (m t) -> p t m", t=PACK)
            )
            return tile

        def interleave(name, planes, shares):
            tile = keep.tile([P, S, PACK], BF16, name=name, align_bytes=64)
            for copy, cols in shares:
                copy(
                    tile[:, cols, :].rearrange("p (c i) t -> p c t i", i=4),
                    planes[:, :, cols].rearrange("p t (c i) -> p c t i", i=4),
                )
            return tile

        def quantize(name, grouped):
            codes = keep.tile([P, S], U32, name=name + "_codes", align_bytes=64)
            scales = keep.tile([P, S], U8, name=name + "_scales", align_bytes=64)
            nc.vector.quantize_mx(
                out=codes[:].bitcast(FP8X4), scales=scales[:], in_=grouped[:].rearrange("p c t -> p (c t)")
            )
            return codes, scales

        def product(bank, lhs, t, rhs, start, stop):
            cols = slice(t * P, (t + 1) * P)
            nc.tensor.matmul_mx(
                out=bank[:],
                lhsT=lhs[0][:, cols].bitcast(FP8X4),
                lhsT_scale=lhs[1][:, cols],
                rhs=rhs[0][:].bitcast(FP8X4),
                rhs_scale=rhs[1][:],
                start=start,
                stop=stop,
            )

        on_scalar = [(nc.scalar.copy, slice(0, S))]
        on_vector = [(nc.vector.tensor_copy, slice(0, S))]
        on_both = [(nc.vector.tensor_copy, slice(0, SPLIT)), (nc.scalar.copy, slice(SPLIT, S))]

        d_scale_table = zeroed_bytes("d_scale_table", G, nc.gpsimd)
        x_scale_table = zeroed_bytes("x_scale_table", T, nc.gpsimd)
        key_scales = zeroed_bytes("key_scales", H, nc.gpsimd)
        two_t = load_list("two_t", two)
        k1_t = load_list("k1_t", k1)
        x_table = load_words("x_table", x_words, T)
        nc.sync.dma_start(d_scale_table[0:P:8, :].bitcast(I32), d_scales[0].bitcast(I32))
        d_table = load_words("d_table", d_words, G)
        for q in range(4):
            nc.scalar.dma_start(
                x_scale_table[32 * q : 32 * q + 4, :].bitcast(I32), x_scales[0, 4 * q : 4 * q + 4, :].bitcast(I32)
            )
        sigmoid_warm = keep.tile([P, 2], F32, name="sigmoid_warm")
        nc.gpsimd.memset(sigmoid_warm[:, 0:1], 0.0)
        nc.scalar.activation(sigmoid_warm[:, 1:2], sigmoid_warm[:, 0:1], ACT.Sigmoid)
        w1_raw = load_weight("w1_raw", w1)
        offs_t = load_list("offs_t", offs)
        n3_t = load_list("n3_t", n3)
        n4_t = load_list("n4_t", n4)

        key_scales_dealt = deal("key_scales_dealt", gather("key_scales_picked", d_scale_table, k1_t, U8), U8)
        for r in range(4):
            nc.scalar.dma_start(
                key_scales[r:P:32, :].bitcast(I32), key_scales_dealt[8 * r : P : 32, :].bitcast(I32)
            )
        w2_raw = load_weight("w2_raw", w2, tag="key_scales_picked")
        n1_t = load_list("n1_t", n1)
        sl_t = load_rows("sl_t", sl)
        th_t = load_rows("th_t", th)
        n2_t = load_list("n2_t", n2)
        gn_t = load_rows("gn_t", gn)
        gm_t = load_rows("gm_t", gm)
        n5_t = load_list("n5_t", n5)
        keys = (deal("key_codes", gather("key_codes_picked", d_table, k1_t, U32), U32), key_scales)
        xb = (gather("xb_codes", x_table, two_t, U32), gather("xb_scales", x_scale_table, two_t, U8))
        b_banks = [psum.tile([P, S], F32, name=f"b_bank{t}", tag=f"late{t}") for t in range(PACK)]
        for t in range(PACK):
            product(b_banks[t], keys, t, xb, True, True)
        xa = (
            gather("xa_codes", x_table, offs_t, U32, tag="key_codes_picked"),
            gather("xa_scales", x_scale_table, offs_t, U8, tag="key_scales_dealt"),
        )
        a_banks = [psum.tile([P, S], F32, name=f"a_bank{t}") for t in range(PACK)]
        for t in range(PACK):
            product(a_banks[t], keys, t, xa, True, True)

        w1_grouped = interleave("w1_grouped", w1_raw, on_scalar)

        sg_bias = keep.tile([P, PACK], F32, name="sg_bias")
        nc.vector.scalar_tensor_tensor(sg_bias[:], sl_t[:], -1.0, th_t[:], ALU.mult, ALU.mult)
        z_gain = keep.tile([P, PACK], F32, name="z_gain")
        nc.vector.tensor_scalar(z_gain[:], gn_t[:], SCORE_SCALE, None, ALU.mult)

        z_planes = keep.tile([P, PACK, S], BF16, name="z_planes", align_bytes=64)
        z2_planes = keep.tile([P, PACK, S], BF16, name="z2_planes", align_bytes=64)

        def rows(name, shape):
            return [keep.tile([P] + shape, F32, name=f"{name}{t}") for t in range(PACK)]

        b_row, pair, lead, share = rows("b_row", [S]), rows("pair", [2, W]), rows("lead", [W]), rows("share", [2, W])
        won, dt = rows("won", [2, W]), rows("dt", [S])
        a_row, st, sg = rows("a_row", [S + SPARE]), rows("st", [2 * S]), rows("sg", [S])

        def fetch_pairs(t):
            nc.scalar.activation(b_row[t][:], b_banks[t][:], ACT.Copy, scale=SCORE_SCALE)
            for half, offsets in enumerate((n3_t, n4_t)):
                if t == 0:
                    nc.scalar.activation(pair[t][:, half, :], b_row[t][:].indirect(offsets[:]), ACT.Copy)
                else:
                    nc.vector.tensor_copy(pair[t][:, half, :], b_row[t][:].indirect(offsets[:]))

        def weigh_pairs(t):
            nc.vector.tensor_tensor(lead[t][:], pair[t][:, 0, :], pair[t][:, 1, :], ALU.subtract)
            nc.scalar.activation(share[t][:, 0, :], lead[t][:], ACT.Sigmoid)
            nc.scalar.activation(share[t][:, 1, :], lead[t][:], ACT.Sigmoid, scale=-1.0)

        def place_pairs(t):
            if t == 0:
                nc.vector.tensor_tensor(won[t][:], pair[t][:], share[t][:], ALU.mult)
                nc.scalar.activation(dt[t][:].indirect(n3_t[:]), won[t][:, 0, :], ACT.Copy)
            else:
                nc.vector.tensor_tensor(won[t][:, 1, :], pair[t][:, 1, :], share[t][:, 1, :], ALU.mult)
                nc.vector.tensor_tensor(dt[t][:].indirect(n3_t[:]), pair[t][:, 0, :], share[t][:, 0, :], ALU.mult)
            nc.scalar.activation(dt[t][:].indirect(n4_t[:]), won[t][:, 1, :], ACT.Copy)

        def round_z2(t):
            nc.vector.tensor_scalar(z2_planes[:, t, :], dt[t][:], gm_t[:, t : t + 1], None, ALU.mult)

        def make_st(t):
            nc.scalar.activation(a_row[t][:, :S], a_banks[t][:], ACT.Copy, scale=SCORE_SCALE)
            nc.vector.tensor_copy(st[t][:, S:], a_row[t][:].indirect(n1_t[:]))
            nc.vector.scalar_tensor_tensor(
                st[t][:, :S], a_banks[t][:], SCORE_SCALE, st[t][:, S:], ALU.mult, ALU.subtract
            )

        def make_sg(t):
            nc.scalar.activation(
                sg[t][:], st[t][:].indirect(n2_t[:]), ACT.Sigmoid, bias=sg_bias[:, t : t + 1], scale=sl_t[:, t : t + 1]
            )

        def round_z(t):
            nc.vector.scalar_tensor_tensor(
                z_planes[:, t, :], a_banks[t][:], z_gain[:, t : t + 1], sg[t][:], ALU.mult, ALU.mult
            )

        b_stages = list(enumerate((fetch_pairs, weigh_pairs, place_pairs, round_z2)))
        a_stages = list(enumerate((make_st, make_sg, round_z), A_LAG))
        for step in range(A_LAG + 2 * PACK - 2):
            for lag, stage in a_stages + b_stages:
                if 0 <= step - lag < PACK:
                    stage(step - lag)
            if step == 2:
                w1_q = quantize("w1", w1_grouped)
                w2_q = quantize("w2", interleave("w2_grouped", w2_raw, on_scalar))
            if step == 2 * PACK - 2:
                z2_q = quantize("z2", interleave("z2_grouped", z2_planes, on_both))

        z_grouped = interleave("z_grouped", z_planes, on_both)
        root_warm = keep.tile([P, 1], F32, name="root_warm")
        nc.scalar.activation(root_warm[:], z_grouped[:, S - 1, 0:1], ACT.Abs_reciprocal_sqrt, bias=0.5, scale=0.0)
        z_q = quantize("z", z_grouped)

        h_banks = [psum.tile([P, S], F32, name=f"h_bank{t}", tag=f"late{t}") for t in range(PACK)]
        for t in range(PACK):
            product(h_banks[t], w2_q, t, z2_q, True, False)
        for t in range(PACK):
            product(h_banks[t], w1_q, t, z_q, False, True)

        size, picked = rows("size", [S + SPARE]), rows("picked", [S])
        root, inverse, result = rows("root", [S]), rows("inverse", [S]), rows("result", [S])
        for t in range(PACK):
            nc.scalar.activation(size[t][:, :S], h_banks[t][:], ACT.Abs)
        pieces = [(t, slice(0, S)) for t in range(PACK - 1)] + [(PACK - 1, slice(0, W)), (PACK - 1, slice(W, S))]
        for t, cols in pieces:
            offsets = n5_t[:, cols.start // 16 : cols.stop // 16]
            nc.vector.tensor_copy(picked[t][:, cols], size[t][:].indirect(offsets))
        for t, cols in pieces:
            nc.scalar.activation(root[t][:, cols], picked[t][:, cols], ACT.Abs_reciprocal_sqrt, bias=0.5)
            nc.scalar.activation(inverse[t][:, cols], root[t][:, cols], ACT.Square)
        for t, cols in pieces:
            nc.vector.tensor_tensor(result[t][:, cols], h_banks[t][:, cols], inverse[t][:, cols], ALU.mult)
            nc.sync.dma_start(out[t * P : (t + 1) * P, cols], result[t][:, cols])
